import numpy as np
import ml_dtypes


def mxq(x, axis, fmt="e4m3"):
    dtype, down = {"e4m3": (ml_dtypes.float8_e4m3fn, 7), "e5m2": (ml_dtypes.float8_e5m2, 14)}[fmt]
    v = np.moveaxis(np.asarray(x, np.float32).astype(ml_dtypes.bfloat16).astype(np.float64), axis, -1)
    blocks = v.reshape(v.shape[:-1] + (-1, 32))
    amax = np.abs(blocks).max(-1, keepdims=True)
    byte = np.maximum(np.where(amax > 0, np.frexp(amax)[1] - 1 + 127, 0) - down, 1)
    scale = np.exp2(byte - 127.0)
    codes = (blocks / scale).astype(np.float32).astype(dtype).astype(np.float64)
    return np.moveaxis((codes * scale).reshape(v.shape), -1, axis)


WIDE = False


def mx_kscale(k):
    if not WIDE:
        return np.ones(k)
    levels = np.array([10, -10, 5, -5, 0])
    if k % 512:
        return np.exp2(np.random.permutation(np.resize(levels, k // 32))).repeat(32)
    a = np.empty((k // 512, 16))
    for p in range(k // 512):
        a[p, :8] = np.random.permutation(np.resize(levels, 8))
        for g in range(8):
            far = levels[np.abs(levels - a[p, g]) >= 10]
            a[p, g + 8] = far[np.random.randint(len(far))]
    return np.exp2(a.ravel()).repeat(32)


def f64(x):
    return np.asarray(x).astype(np.float64)


def striped(idx):
    return np.tile(idx.reshape(-1, 16).T, (8, 1)).astype(np.uint16)


def unstriped(offs):
    return offs[:16].T.reshape(-1).astype(np.int64)


E2M1 = np.array([0.0, 0.5, 1.0, 1.5, 2.0, 3.0, 4.0, 6.0, -0.0, -0.5, -1.0, -1.5, -2.0, -3.0, -4.0, -6.0])


def pack_weight(w, fmt):
    k, n = w.shape
    w = f64(np.asarray(w, np.float32).astype(ml_dtypes.bfloat16)).reshape(k // 32, 32, n)
    amax = np.abs(w).max(1)
    if fmt == "e4m3":
        byte = np.frexp(amax)[1] - 1 + 127 - 7
    else:
        mant, ex = np.frexp(amax / 6.0)
        byte = np.where(mant > 0.5, ex, ex - 1) + 127
    byte = np.clip(np.where(amax > 0, byte, 1), 1, 254)
    scaled = (w * np.exp2(127.0 - byte)[:, None, :]).reshape(k, n).astype(np.float32)
    by_word = np.ascontiguousarray(scaled.reshape(k // 512, 128, 4, n).transpose(0, 1, 3, 2))
    if fmt == "e4m3":
        words = by_word.astype(ml_dtypes.float8_e4m3fn).view(np.uint8)
    else:
        c = by_word.astype(ml_dtypes.float4_e2m1fn).view(np.uint8) & 0xF
        words = (c[..., 0::2] | (c[..., 1::2] << 4)).reshape(k // 512, 128, 2 * n)
    return np.ascontiguousarray(words), np.ascontiguousarray(byte.astype(np.uint8).reshape(k // 512, 16, n))


def unpack_weight(words, scales, fmt):
    g, _, n = scales.shape
    words = np.ascontiguousarray(words).reshape(g, 128, n, -1)
    if fmt == "e4m3":
        vals = words.view(ml_dtypes.float8_e4m3fn).astype(np.float64)
    else:
        nib = np.empty((g, 128, n, 4), np.uint8)
        nib[..., 0::2] = words & 0xF
        nib[..., 1::2] = words >> 4
        vals = E2M1[nib]
    vals = vals * np.repeat(np.exp2(scales.astype(np.float64) - 127.0), 8, axis=1)[..., None]
    return vals.transpose(0, 1, 3, 2).reshape(g * 512, n)


def d_relu(v):
    return (v > 0).astype(np.float64)


K, T, E, C, H, N = 256, 1024, 8, 128, 512, 1024


def by_expert(wq, xq):
    return np.concatenate([wq[e].T @ xq[:, e * C:(e + 1) * C] for e in range(E)], axis=1)


def setup_inputs():
    n = np.random.standard_normal
    v = mx_kscale(N)
    u = mx_kscale(H)
    slot_token = np.random.permutation(T)[:E * C]
    w_slot = np.random.uniform(0.2, 1.0, E * C)
    dy = pack_weight(n((N, T)) * v[:, None], "e4m3")
    w2t = pack_weight(n((N, H)) / np.sqrt(N) / v[:, None] * u, "e4m3")
    w1t = [pack_weight(m, "e4m3") for m in n((E, H, K)) / np.sqrt(H) / u[None, :, None]]
    return {
        "dy_words": dy[0],
        "dy_scales": dy[1],
        "w2t_words": w2t[0],
        "w2t_scales": w2t[1],
        "w1t_words": np.stack([m[0] for m in w1t]),
        "w1t_scales": np.stack([m[1] for m in w1t]),
        "a": (n((H, E * C))).astype(np.float32),
        "gate": (np.tile(w_slot, (128, 1))).astype(np.float32),
        "offs": striped(slot_token),
    }


def reference(dy_words, dy_scales, w2t_words, w2t_scales, w1t_words, w1t_scales, a, gate, offs):
    w2t = unpack_weight(w2t_words, w2t_scales, "e4m3")
    w1t = np.stack([unpack_weight(w1t_words[e], w1t_scales[e], "e4m3") for e in range(E)])
    idx = unstriped(offs)
    dc = w2t.T @ unpack_weight(dy_words, dy_scales, "e4m3")
    da = f64(gate[:1]) * dc[:, idx] * d_relu(f64(a))
    dx = by_expert(w1t, mxq(da, 0, "e4m3"))
    out = np.zeros((K, T))
    out[:, idx] = dx
    return out

@@ -1,0 +1,195 @@
+from contextlib import ExitStack
+
+import concourse.mybir as mybir
+
+K, T, E, C, H, N = 256, 1024, 8, 128, 512, 1024
+FLOPS = 2 * N * H * T + 2 * H * K * E * C
+
+F32 = mybir.dt.float32
+BF16 = mybir.dt.bfloat16
+I32 = mybir.dt.int32
+U8 = mybir.dt.uint8
+U16 = mybir.dt.uint16
+FP8X4 = mybir.dt.float8_e4m3fn_x4
+ALU = mybir.AluOpType
+ACT = mybir.ActivationFunctionType
+
+P = 128
+PACK = 4
+PASSES = N // (P * PACK)
+BANK = 512
+HALVES = T // BANK
+CHUNK = 256
+CHUNKS = E * C // CHUNK
+EXPERTS_PER_CHUNK = CHUNK // C
+K_BLOCKS = K // P
+LIST_COLS = CHUNK // 16
+
+
+def tile_moe_sdb_relu_kernel(
+    tc, dy_words, dy_scales, w2t_words, w2t_scales, w1t_words, w1t_scales, a, gate, offs, out
+):
+    nc = tc.nc
+    with ExitStack() as ctx:
+        lists = ctx.enter_context(tc.tile_pool(name="lists", bufs=1))
+        sb = ctx.enter_context(tc.tile_pool(name="sb", bufs=1))
+        psum = ctx.enter_context(tc.psum_pool(name="psum", bufs=2))
+
+        w2_sc_raw = sb.tile([P, PASSES, H], U8, name="w2_sc_raw", align_bytes=64)
+        dy_sc = sb.tile([P, PASSES, T], U8, name="dy_sc", align_bytes=64)
+        w1_sc = sb.tile([P, E, K], U8, name="w1_sc", align_bytes=64)
+        nc.vector.memset(w2_sc_raw[:].bitcast(I32), 0)
+        nc.vector.memset(dy_sc[:].bitcast(I32), 0)
+        nc.vector.memset(w1_sc[:].bitcast(I32), 0)
+
+        w2_rows = w2t_scales.rearrange("s (q r) i -> r q s i", r=4)
+        dy_rows = dy_scales.rearrange("s (q r) t -> r q s t", r=4)
+        w1_rows = w1t_scales.rearrange("e o (q r) k -> r q (e o) k", r=4)
+
+        def load_scale_rows(queue, plane, rows, r):
+            queue.dma_start(plane[r:P:32, :, :].bitcast(I32), rows[r].bitcast(I32))
+
+        def load_dy(s):
+            dy_s = sb.tile([P, T], I32, name=f"dy{s}", align_bytes=64)
+            nc.sync.dma_start(dy_s[:], dy_words[s].rearrange("p t d -> p (t d)").bitcast(I32))
+            return dy_s
+
+        def load_a(c):
+            a_c = sb.tile([P, PACK, CHUNK], F32, name=f"a{c}", align_bytes=64)
+            nc.sync.dma_start(a_c[:], a.rearrange("(p d) j -> p d j", d=PACK)[:, :, c * CHUNK : (c + 1) * CHUNK])
+            return a_c
+
+        def load_w1(g):
+            w1_g = sb.tile([P, E // 2, K], I32, name=f"w1_{g}", align_bytes=64)
+            words = w1t_words[g * (E // 2) : (g + 1) * (E // 2)]
+            nc.sync.dma_start(w1_g[:], words.rearrange("e o p k d -> p (e o) (k d)").bitcast(I32))
+            return w1_g
+
+        offsets = lists.tile([P, E * C // 16], U16, name="offsets")
+        nc.sync.dma_start(offsets[:], offs)
+        w2_raw = sb.tile([P, PASSES, H], I32, name="w2_raw", align_bytes=64)
+        nc.sync.dma_start(w2_raw[:], w2t_words.rearrange("s p i d -> p s (i d)").bitcast(I32))
+        for r in range(4):
+            load_scale_rows(nc.scalar, w2_sc_raw, w2_rows, r)
+        dy = [load_dy(0)]
+        load_scale_rows(nc.sync, dy_sc, dy_rows, 0)
+        dy.append(load_dy(1))
+        for r in range(1, 4):
+            load_scale_rows(nc.scalar, dy_sc, dy_rows, r)
+        gate_sb = sb.tile([P, E * C], F32, name="gate_sb", align_bytes=64)
+        nc.sync.dma_start(gate_sb[:], gate)
+        a_sb = [load_a(0), load_a(1)]
+        w1 = [load_w1(0)]
+        for r in range(4):
+            load_scale_rows(nc.sync, w1_sc, w1_rows, r)
+        a_sb.extend([load_a(2), load_a(3)])
+        w1.append(load_w1(1))
+
+        w2_sc = sb.tile([P, PACK, PASSES, P], U8, name="w2_sc", align_bytes=64)
+        nc.vector.tensor_copy(w2_sc[:], w2_sc_raw[:].rearrange("p s (m d) -> p d s m", d=PACK))
+        w2 = []
+        for d in range(PACK):
+            w2_d = sb.tile([P, PASSES, P], I32, name=f"w2_{d}", align_bytes=64)
+            nc.vector.tensor_copy(w2_d[:], w2_raw[:].rearrange("p s (m d) -> p d s m", d=PACK)[:, d])
+            w2.append(w2_d)
+
+        dc = []
+        for d in range(PACK):
+            dc_d = sb.tile([P, T], F32, name=f"dc{d}", align_bytes=64)
+            for h in range(HALVES):
+                cols = slice(h * BANK, (h + 1) * BANK)
+                acc = psum.tile([P, BANK], F32, name="acc")
+                for s in range(PASSES):
+                    nc.tensor.matmul_mx(
+                        out=acc[:],
+                        lhsT=w2[d][:, s, :].bitcast(FP8X4),
+                        lhsT_scale=w2_sc[:, d, s, :],
+                        rhs=dy[s][:, cols].bitcast(FP8X4),
+                        rhs_scale=dy_sc[:, s, cols],
+                        start=(s == 0),
+                        stop=(s == PASSES - 1),
+                    )
+                if d == 0:
+                    nc.vector.tensor_copy(dc_d[:, cols], acc[:])
+                else:
+                    nc.scalar.copy(dc_d[:, cols], acc[:])
+            dc.append(dc_d)
+
+        gathered = [
+            sb.tile([P, PACK, CHUNK], F32, name=f"gathered{c}", tag=f"gathered_then_dx{c}", align_bytes=64)
+            for c in range(CHUNKS)
+        ]
+        for d in range(PACK):
+            for c in range(CHUNKS):
+                nc.vector.tensor_tensor(
+                    gathered[c][:, d, :],
+                    dc[d][:].indirect(offsets[:, c * LIST_COLS : (c + 1) * LIST_COLS]),
+                    gate_sb[:, c * CHUNK : (c + 1) * CHUNK],
+                    ALU.mult,
+                )
+
+        out_sb = [sb.tile([P, T], F32, name=f"out_sb{kb}", align_bytes=64) for kb in range(K_BLOCKS)]
+
+        def woven(tile_ap):
+            return tile_ap.rearrange("p (g i) d -> p g d i", i=4)
+
+        def planes(tile_ap):
+            return tile_ap.rearrange("p d (g i) -> p g d i", i=4)
+
+        def make_sign(c):
+            sgn = sb.tile([P, CHUNK, PACK], BF16, name=f"sgn{c}", align_bytes=64)
+            nc.scalar.activation(woven(sgn[:]), planes(a_sb[c][:]), ACT.Sign)
+            return sgn
+
+        def make_mask(c, sgn):
+            mask = sb.tile([P, CHUNK, PACK], BF16, name=f"mask{c}", align_bytes=64)
+            nc.scalar.activation(mask[:], sgn[:], ACT.Relu)
+            return mask
+
+        def first_half(c, mask):
+            rounded = sb.tile([P, CHUNK, PACK], BF16, name=f"rounded{c}", align_bytes=64)
+            nc.scalar.copy(woven(rounded[:]), planes(gathered[c][:]))
+            da = sb.tile([P, CHUNK, PACK], BF16, name=f"da{c}", align_bytes=64)
+            nc.vector.tensor_tensor(da[:], rounded[:], mask[:], ALU.mult)
+            codes = sb.tile([P, CHUNK], I32, name=f"codes{c}", align_bytes=64)
+            scales = sb.tile([P, CHUNK], U8, name=f"scales{c}", align_bytes=64)
+            nc.vector.quantize_mx(
+                out=codes[:].bitcast(FP8X4), scales=scales[:], in_=da[:].rearrange("p j d -> p (j d)")
+            )
+            acc = psum.tile([P, K_BLOCKS, CHUNK], F32, name="acc_dx", bufs=4)
+            for kb in range(K_BLOCKS):
+                for u in range(EXPERTS_PER_CHUNK):
+                    e = c * EXPERTS_PER_CHUNK + u
+                    nc.tensor.matmul_mx(
+                        out=acc[:, kb, u * C : (u + 1) * C],
+                        lhsT=w1[e // (E // 2)][:, e % (E // 2), kb * P : (kb + 1) * P].bitcast(FP8X4),
+                        lhsT_scale=w1_sc[:, e, kb * P : (kb + 1) * P],
+                        rhs=codes[:, u * C : (u + 1) * C].bitcast(FP8X4),
+                        rhs_scale=scales[:, u * C : (u + 1) * C],
+                        start=True,
+                        stop=True,
+                    )
+            return acc
+
+        def second_half(c, acc):
+            dx = sb.tile(
+                [P, K_BLOCKS, CHUNK], F32, name=f"dx{c}", tag=f"gathered_then_dx{(c + 1) % CHUNKS}", align_bytes=64
+            )
+            nc.scalar.copy(dx[:], acc[:])
+            for kb in range(K_BLOCKS):
+                nc.vector.tensor_copy(
+                    out_sb[kb][:].indirect(offsets[:, c * LIST_COLS : (c + 1) * LIST_COLS]), dx[:, kb, :]
+                )
+
+        sgn0 = make_sign(0)
+        sgn1 = make_sign(1)
+        mask0 = make_mask(0, sgn0)
+        accs = [first_half(0, mask0)]
+        accs.append(first_half(1, make_mask(1, sgn1)))
+        second_half(0, accs[0])
+        for c in range(2, CHUNKS):
+            accs.append(first_half(c, make_mask(c, make_sign(c))))
+            second_half(c - 1, accs[c - 1])
+        second_half(CHUNKS - 1, accs[CHUNKS - 1])
+        for kb in range(K_BLOCKS):
+            nc.sync.dma_start(out[kb * P : (kb + 1) * P, :], out_sb[kb][:])

@@ -33,12 +33,12 @@ def tile_moe_sdb_relu_kernel(
     with ExitStack() as ctx:
         lists = ctx.enter_context(tc.tile_pool(name="lists", bufs=1))
         sb = ctx.enter_context(tc.tile_pool(name="sb", bufs=1))
-        psum = ctx.enter_context(tc.psum_pool(name="psum", bufs=2))
+        psum = ctx.enter_context(tc.psum_pool(name="psum", bufs=4))
 
         w2_sc_raw = sb.tile([P, PASSES, H], U8, name="w2_sc_raw", align_bytes=64)
         dy_sc = sb.tile([P, PASSES, T], U8, name="dy_sc", align_bytes=64)
         w1_sc = sb.tile([P, E, K], U8, name="w1_sc", align_bytes=64)
-        nc.vector.memset(w2_sc_raw[:].bitcast(I32), 0)
+        nc.gpsimd.memset(w2_sc_raw[:].bitcast(I32), 0)
         nc.vector.memset(dy_sc[:].bitcast(I32), 0)
         nc.vector.memset(w1_sc[:].bitcast(I32), 0)
 
@@ -48,11 +48,6 @@ def tile_moe_sdb_relu_kernel(
 
         def load_scale_rows(queue, plane, rows, r):
             queue.dma_start(plane[r:P:32, :, :].bitcast(I32), rows[r].bitcast(I32))
-
-        def load_dy(s):
-            dy_s = sb.tile([P, T], I32, name=f"dy{s}", align_bytes=64)
-            nc.sync.dma_start(dy_s[:], dy_words[s].rearrange("p t d -> p (t d)").bitcast(I32))
-            return dy_s
 
         def load_a(c):
             a_c = sb.tile([P, PACK, CHUNK], F32, name=f"a{c}", align_bytes=64)
@@ -70,29 +65,44 @@ def tile_moe_sdb_relu_kernel(
         w2_raw = sb.tile([P, PASSES, H], I32, name="w2_raw", align_bytes=64)
         nc.sync.dma_start(w2_raw[:], w2t_words.rearrange("s p i d -> p s (i d)").bitcast(I32))
         for r in range(4):
-            load_scale_rows(nc.scalar, w2_sc_raw, w2_rows, r)
-        dy = [load_dy(0)]
-        load_scale_rows(nc.sync, dy_sc, dy_rows, 0)
-        dy.append(load_dy(1))
-        for r in range(1, 4):
-            load_scale_rows(nc.scalar, dy_sc, dy_rows, r)
-        gate_sb = sb.tile([P, E * C], F32, name="gate_sb", align_bytes=64)
-        nc.sync.dma_start(gate_sb[:], gate)
-        a_sb = [load_a(0), load_a(1)]
+            load_scale_rows(nc.sync, w2_sc_raw, w2_rows, r)
+        dy = sb.tile([P, PASSES, T], I32, name="dy", align_bytes=64)
+        nc.sync.dma_start(dy[:], dy_words.rearrange("s p t d -> p s (t d)").bitcast(I32))
+        for r in range(4):
+            load_scale_rows(nc.sync, dy_sc, dy_rows, r)
+        gate_first = sb.tile([P, CHUNK], F32, name="gate_first", align_bytes=64)
+        nc.sync.dma_start(gate_first[:], gate[:, 0:CHUNK])
+        a_sb = [load_a(0)]
+        gate_rest = sb.tile([P, E * C - CHUNK], F32, name="gate_rest", align_bytes=64)
+        nc.sync.dma_start(gate_rest[:], gate[:, CHUNK : E * C])
+        a_sb.extend([load_a(1), load_a(2)])
         w1 = [load_w1(0)]
         for r in range(4):
             load_scale_rows(nc.sync, w1_sc, w1_rows, r)
-        a_sb.extend([load_a(2), load_a(3)])
+        a_sb.append(load_a(3))
         w1.append(load_w1(1))
 
-        w2_sc = sb.tile([P, PACK, PASSES, P], U8, name="w2_sc", align_bytes=64)
-        nc.vector.tensor_copy(w2_sc[:], w2_sc_raw[:].rearrange("p s (m d) -> p d s m", d=PACK))
         w2 = []
+        w2_sc = []
         for d in range(PACK):
             w2_d = sb.tile([P, PASSES, P], I32, name=f"w2_{d}", align_bytes=64)
             nc.vector.tensor_copy(w2_d[:], w2_raw[:].rearrange("p s (m d) -> p d s m", d=PACK)[:, d])
             w2.append(w2_d)
+            w2_sc_d = sb.tile([P, PASSES, P], U8, name=f"w2_sc_{d}", align_bytes=64)
+            nc.vector.tensor_copy(w2_sc_d[:], w2_sc_raw[:].rearrange("p s (m d) -> p d s m", d=PACK)[:, d])
+            w2_sc.append(w2_sc_d)
 
+        warm = psum.tile([P, BANK], F32, name="acc_dx")
+        for s in range(PASSES):
+            nc.tensor.matmul_mx(
+                out=warm[:],
+                lhsT=w2_raw[:, s, 0:P].bitcast(FP8X4),
+                lhsT_scale=w2_sc_raw[:, s, 0:P],
+                rhs=w2_raw[:, s, :].bitcast(FP8X4),
+                rhs_scale=w2_sc_raw[:, s, :],
+                start=True,
+                stop=True,
+            )
         dc = []
         for d in range(PACK):
             dc_d = sb.tile([P, T], F32, name=f"dc{d}", align_bytes=64)
@@ -103,32 +113,14 @@ def tile_moe_sdb_relu_kernel(
                     nc.tensor.matmul_mx(
                         out=acc[:],
                         lhsT=w2[d][:, s, :].bitcast(FP8X4),
-                        lhsT_scale=w2_sc[:, d, s, :],
-                        rhs=dy[s][:, cols].bitcast(FP8X4),
+                        lhsT_scale=w2_sc[d][:, s, :],
+                        rhs=dy[:, s, cols].bitcast(FP8X4),
                         rhs_scale=dy_sc[:, s, cols],
                         start=(s == 0),
                         stop=(s == PASSES - 1),
                     )
-                if d == 0:
-                    nc.vector.tensor_copy(dc_d[:, cols], acc[:])
-                else:
-                    nc.scalar.copy(dc_d[:, cols], acc[:])
+                nc.scalar.copy(dc_d[:, cols], acc[:])
             dc.append(dc_d)
-
-        gathered = [
-            sb.tile([P, PACK, CHUNK], F32, name=f"gathered{c}", tag=f"gathered_then_dx{c}", align_bytes=64)
-            for c in range(CHUNKS)
-        ]
-        for d in range(PACK):
-            for c in range(CHUNKS):
-                nc.vector.tensor_tensor(
-                    gathered[c][:, d, :],
-                    dc[d][:].indirect(offsets[:, c * LIST_COLS : (c + 1) * LIST_COLS]),
-                    gate_sb[:, c * CHUNK : (c + 1) * CHUNK],
-                    ALU.mult,
-                )
-
-        out_sb = [sb.tile([P, T], F32, name=f"out_sb{kb}", align_bytes=64) for kb in range(K_BLOCKS)]
 
         def woven(tile_ap):
             return tile_ap.rearrange("p (g i) d -> p g d i", i=4)
@@ -137,7 +129,7 @@ def tile_moe_sdb_relu_kernel(
             return tile_ap.rearrange("p d (g i) -> p g d i", i=4)
 
         def make_sign(c):
-            sgn = sb.tile([P, CHUNK, PACK], BF16, name=f"sgn{c}", align_bytes=64)
+            sgn = sb.tile([P, CHUNK, PACK], BF16, name=f"sgn{c}", tag=f"gathered_then_dx{c + 2}", align_bytes=64)
             nc.scalar.activation(woven(sgn[:]), planes(a_sb[c][:]), ACT.Sign)
             return sgn
 
@@ -146,17 +138,39 @@ def tile_moe_sdb_relu_kernel(
             nc.scalar.activation(mask[:], sgn[:], ACT.Relu)
             return mask
 
+        mask1 = make_mask(1, make_sign(1))
+        gathered = [
+            sb.tile([P, PACK, CHUNK], F32, name=f"gathered{c}", tag=f"gathered_then_dx{c}", align_bytes=64)
+            for c in range(CHUNKS)
+        ]
+        gated = sb.tile([P, PACK, CHUNK], F32, name="gated", align_bytes=64)
+        for d in range(PACK):
+            nc.vector.scalar_tensor_tensor(gated[:, d, :], a_sb[0][:, d, :], 0.0, gate_first[:], ALU.is_gt, ALU.mult)
+        for d in range(PACK):
+            for c in range(CHUNKS):
+                factor = gated[:, d, :] if c == 0 else gate_rest[:, (c - 1) * CHUNK : c * CHUNK]
+                nc.vector.tensor_tensor(
+                    gathered[c][:, d, :],
+                    dc[d][:].indirect(offsets[:, c * LIST_COLS : (c + 1) * LIST_COLS]),
+                    factor,
+                    ALU.mult,
+                )
+
+        out_sb = [sb.tile([P, T], F32, name=f"out_sb{kb}", align_bytes=64) for kb in range(K_BLOCKS)]
+
         def first_half(c, mask):
-            rounded = sb.tile([P, CHUNK, PACK], BF16, name=f"rounded{c}", align_bytes=64)
+            rounded = sb.tile([P, CHUNK, PACK], BF16, name=f"rounded{c}", tag=f"rounded_then_dx{c}", align_bytes=64)
             nc.scalar.copy(woven(rounded[:]), planes(gathered[c][:]))
-            da = sb.tile([P, CHUNK, PACK], BF16, name=f"da{c}", align_bytes=64)
-            nc.vector.tensor_tensor(da[:], rounded[:], mask[:], ALU.mult)
+            da = rounded
+            if mask is not None:
+                da = sb.tile([P, CHUNK, PACK], BF16, name=f"da{c}", align_bytes=64)
+                nc.vector.tensor_tensor(da[:], rounded[:], mask[:], ALU.mult)
             codes = sb.tile([P, CHUNK], I32, name=f"codes{c}", align_bytes=64)
             scales = sb.tile([P, CHUNK], U8, name=f"scales{c}", align_bytes=64)
             nc.vector.quantize_mx(
                 out=codes[:].bitcast(FP8X4), scales=scales[:], in_=da[:].rearrange("p j d -> p (j d)")
             )
-            acc = psum.tile([P, K_BLOCKS, CHUNK], F32, name="acc_dx", bufs=4)
+            acc = psum.tile([P, K_BLOCKS, CHUNK], F32, name="acc_dx")
             for kb in range(K_BLOCKS):
                 for u in range(EXPERTS_PER_CHUNK):
                     e = c * EXPERTS_PER_CHUNK + u
@@ -172,24 +186,23 @@ def tile_moe_sdb_relu_kernel(
             return acc
 
         def second_half(c, acc):
-            dx = sb.tile(
-                [P, K_BLOCKS, CHUNK], F32, name=f"dx{c}", tag=f"gathered_then_dx{(c + 1) % CHUNKS}", align_bytes=64
-            )
-            nc.scalar.copy(dx[:], acc[:])
-            for kb in range(K_BLOCKS):
-                nc.vector.tensor_copy(
-                    out_sb[kb][:].indirect(offsets[:, c * LIST_COLS : (c + 1) * LIST_COLS]), dx[:, kb, :]
+            for kb, held in enumerate(("gathered", "rounded")):
+                dx = sb.tile(
+                    [P, CHUNK], F32, name=f"dx{c}_{kb}", tag=f"{held}_then_dx{(c + 1) % CHUNKS}", align_bytes=64
                 )
+                nc.scalar.copy(dx[:], acc[:, kb, :])
+                nc.vector.tensor_copy(out_sb[kb][:].indirect(offsets[:, c * LIST_COLS : (c + 1) * LIST_COLS]), dx[:])
 
-        sgn0 = make_sign(0)
-        sgn1 = make_sign(1)
-        mask0 = make_mask(0, sgn0)
-        accs = [first_half(0, mask0)]
-        accs.append(first_half(1, make_mask(1, sgn1)))
+        accs = [first_half(0, None)]
+        accs.append(first_half(1, mask1))
+        sgn2 = make_sign(2)
         second_half(0, accs[0])
-        for c in range(2, CHUNKS):
-            accs.append(first_half(c, make_mask(c, make_sign(c))))
-            second_half(c - 1, accs[c - 1])
+        mask2 = make_mask(2, sgn2)
+        sgn3 = make_sign(3)
+        accs.append(first_half(2, mask2))
+        second_half(1, accs[1])
+        accs.append(first_half(3, make_mask(3, sgn3)))
+        second_half(2, accs[2])
         second_half(CHUNKS - 1, accs[CHUNKS - 1])
         for kb in range(K_BLOCKS):
             nc.sync.dma_start(out[kb * P : (kb + 1) * P, :], out_sb[kb][:])

@@ -24,6 +24,7 @@ CHUNKS = E * C // CHUNK
 EXPERTS_PER_CHUNK = CHUNK // C
 K_BLOCKS = K // P
 LIST_COLS = CHUNK // 16
+GATHERS = ((0, CHUNK), (CHUNK, CHUNK), (2 * CHUNK, 2 * CHUNK))
 
 
 def tile_moe_sdb_relu_kernel(
@@ -54,6 +55,12 @@ def tile_moe_sdb_relu_kernel(
             nc.sync.dma_start(a_c[:], a.rearrange("(p d) j -> p d j", d=PACK)[:, :, c * CHUNK : (c + 1) * CHUNK])
             return a_c
 
+        def load_gate(n):
+            first, width = GATHERS[n]
+            gate_n = sb.tile([P, width], F32, name=f"gate{n}", align_bytes=64)
+            nc.sync.dma_start(gate_n[:], gate[:, first : first + width])
+            return gate_n
+
         def load_w1(g):
             w1_g = sb.tile([P, E // 2, K], I32, name=f"w1_{g}", align_bytes=64)
             words = w1t_words[g * (E // 2) : (g + 1) * (E // 2)]
@@ -70,12 +77,11 @@ def tile_moe_sdb_relu_kernel(
         nc.sync.dma_start(dy[:], dy_words.rearrange("s p t d -> p s (t d)").bitcast(I32))
         for r in range(4):
             load_scale_rows(nc.sync, dy_sc, dy_rows, r)
-        gate_first = sb.tile([P, CHUNK], F32, name="gate_first", align_bytes=64)
-        nc.sync.dma_start(gate_first[:], gate[:, 0:CHUNK])
+        gates = [load_gate(0)]
         a_sb = [load_a(0)]
-        gate_rest = sb.tile([P, E * C - CHUNK], F32, name="gate_rest", align_bytes=64)
-        nc.sync.dma_start(gate_rest[:], gate[:, CHUNK : E * C])
+        gates.append(load_gate(1))
         a_sb.extend([load_a(1), load_a(2)])
+        gates.append(load_gate(2))
         w1 = [load_w1(0)]
         for r in range(4):
             load_scale_rows(nc.sync, w1_sc, w1_rows, r)
@@ -129,7 +135,7 @@ def tile_moe_sdb_relu_kernel(
             return tile_ap.rearrange("p d (g i) -> p g d i", i=4)
 
         def make_sign(c):
-            sgn = sb.tile([P, CHUNK, PACK], BF16, name=f"sgn{c}", tag=f"gathered_then_dx{c + 2}", align_bytes=64)
+            sgn = sb.tile([P, CHUNK, PACK], BF16, name=f"sgn{c}", align_bytes=64)
             nc.scalar.activation(woven(sgn[:]), planes(a_sb[c][:]), ACT.Sign)
             return sgn
 
@@ -138,29 +144,26 @@ def tile_moe_sdb_relu_kernel(
             nc.scalar.activation(mask[:], sgn[:], ACT.Relu)
             return mask
 
-        mask1 = make_mask(1, make_sign(1))
-        gathered = [
-            sb.tile([P, PACK, CHUNK], F32, name=f"gathered{c}", tag=f"gathered_then_dx{c}", align_bytes=64)
-            for c in range(CHUNKS)
-        ]
         gated = sb.tile([P, PACK, CHUNK], F32, name="gated", align_bytes=64)
         for d in range(PACK):
-            nc.vector.scalar_tensor_tensor(gated[:, d, :], a_sb[0][:, d, :], 0.0, gate_first[:], ALU.is_gt, ALU.mult)
-        for d in range(PACK):
-            for c in range(CHUNKS):
-                factor = gated[:, d, :] if c == 0 else gate_rest[:, (c - 1) * CHUNK : c * CHUNK]
+            nc.vector.scalar_tensor_tensor(gated[:, d, :], a_sb[0][:, d, :], 0.0, gates[0][:], ALU.is_gt, ALU.mult)
+        gathered = []
+        for n, (first, width) in enumerate(GATHERS):
+            g_n = sb.tile([P, PACK, width], F32, name=f"gathered{n}", align_bytes=64)
+            for d in range(PACK):
                 nc.vector.tensor_tensor(
-                    gathered[c][:, d, :],
-                    dc[d][:].indirect(offsets[:, c * LIST_COLS : (c + 1) * LIST_COLS]),
-                    factor,
+                    g_n[:, d, :],
+                    dc[d][:].indirect(offsets[:, first // 16 : (first + width) // 16]),
+                    gated[:, d, :] if n == 0 else gates[n][:],
                     ALU.mult,
                 )
+            gathered.extend(g_n[:, :, j : j + CHUNK] for j in range(0, width, CHUNK))
 
         out_sb = [sb.tile([P, T], F32, name=f"out_sb{kb}", align_bytes=64) for kb in range(K_BLOCKS)]
 
         def first_half(c, mask):
             rounded = sb.tile([P, CHUNK, PACK], BF16, name=f"rounded{c}", tag=f"rounded_then_dx{c}", align_bytes=64)
-            nc.scalar.copy(woven(rounded[:]), planes(gathered[c][:]))
+            nc.scalar.copy(woven(rounded[:]), planes(gathered[c]))
             da = rounded
             if mask is not None:
                 da = sb.tile([P, CHUNK, PACK], BF16, name=f"da{c}", align_bytes=64)
@@ -186,22 +189,24 @@ def tile_moe_sdb_relu_kernel(
             return acc
 
         def second_half(c, acc):
-            for kb, held in enumerate(("gathered", "rounded")):
-                dx = sb.tile(
-                    [P, CHUNK], F32, name=f"dx{c}_{kb}", tag=f"{held}_then_dx{(c + 1) % CHUNKS}", align_bytes=64
-                )
+            for kb in range(K_BLOCKS):
+                tag = f"dx{c}" if kb == 0 else f"rounded_then_dx{(c + 1) % CHUNKS}"
+                dx = sb.tile([P, CHUNK], F32, name=f"dx{c}_{kb}", tag=tag, align_bytes=64)
                 nc.scalar.copy(dx[:], acc[:, kb, :])
                 nc.vector.tensor_copy(out_sb[kb][:].indirect(offsets[:, c * LIST_COLS : (c + 1) * LIST_COLS]), dx[:])
 
+        sgn1 = make_sign(1)
+        sgn2 = make_sign(2)
+        mask1 = make_mask(1, sgn1)
         accs = [first_half(0, None)]
         accs.append(first_half(1, mask1))
-        sgn2 = make_sign(2)
-        second_half(0, accs[0])
         mask2 = make_mask(2, sgn2)
+        second_half(0, accs[0])
         sgn3 = make_sign(3)
         accs.append(first_half(2, mask2))
+        mask3 = make_mask(3, sgn3)
         second_half(1, accs[1])
-        accs.append(first_half(3, make_mask(3, sgn3)))
+        accs.append(first_half(3, mask3))
         second_half(2, accs[2])
         second_half(CHUNKS - 1, accs[CHUNKS - 1])
         for kb in range(K_BLOCKS):

@@ -98,17 +98,6 @@ def tile_moe_sdb_relu_kernel(
             nc.vector.tensor_copy(w2_sc_d[:], w2_sc_raw[:].rearrange("p s (m d) -> p d s m", d=PACK)[:, d])
             w2_sc.append(w2_sc_d)
 
-        warm = psum.tile([P, BANK], F32, name="acc_dx")
-        for s in range(PASSES):
-            nc.tensor.matmul_mx(
-                out=warm[:],
-                lhsT=w2_raw[:, s, 0:P].bitcast(FP8X4),
-                lhsT_scale=w2_sc_raw[:, s, 0:P],
-                rhs=w2_raw[:, s, :].bitcast(FP8X4),
-                rhs_scale=w2_sc_raw[:, s, :],
-                start=True,
-                stop=True,
-            )
         dc = []
         for d in range(PACK):
             dc_d = sb.tile([P, T], F32, name=f"dc{d}", align_bytes=64)
@@ -166,8 +155,9 @@ def tile_moe_sdb_relu_kernel(
             nc.scalar.copy(woven(rounded[:]), planes(gathered[c]))
             da = rounded
             if mask is not None:
-                da = sb.tile([P, CHUNK, PACK], BF16, name=f"da{c}", align_bytes=64)
-                nc.vector.tensor_tensor(da[:], rounded[:], mask[:], ALU.mult)
+                da = sb.tile([P, CHUNK, PACK], BF16, name=f"da{c}", tag="da", align_bytes=64)
+                engine = nc.vector if c == 1 else nc.gpsimd
+                engine.tensor_tensor(da[:], rounded[:], mask[:], ALU.mult)
             codes = sb.tile([P, CHUNK], I32, name=f"codes{c}", align_bytes=64)
             scales = sb.tile([P, CHUNK], U8, name=f"scales{c}", align_bytes=64)
             nc.vector.quantize_mx(
@@ -200,13 +190,10 @@ def tile_moe_sdb_relu_kernel(
         mask1 = make_mask(1, sgn1)
         accs = [first_half(0, None)]
         accs.append(first_half(1, mask1))
-        mask2 = make_mask(2, sgn2)
+        accs.append(first_half(2, make_mask(2, sgn2)))
         second_half(0, accs[0])
-        sgn3 = make_sign(3)
-        accs.append(first_half(2, mask2))
-        mask3 = make_mask(3, sgn3)
+        accs.append(first_half(3, make_mask(3, make_sign(3))))
         second_half(1, accs[1])
-        accs.append(first_half(3, mask3))
         second_half(2, accs[2])
         second_half(CHUNKS - 1, accs[CHUNKS - 1])
         for kb in range(K_BLOCKS):

@@ -98,6 +98,17 @@ def tile_moe_sdb_relu_kernel(
             nc.vector.tensor_copy(w2_sc_d[:], w2_sc_raw[:].rearrange("p s (m d) -> p d s m", d=PACK)[:, d])
             w2_sc.append(w2_sc_d)
 
+        warm = psum.tile([P, BANK], F32, name="acc_dx")
+        for s in range(PASSES):
+            nc.tensor.matmul_mx(
+                out=warm[:],
+                lhsT=w2_raw[:, s, 0:P].bitcast(FP8X4),
+                lhsT_scale=w2_sc_raw[:, s, 0:P],
+                rhs=w2_raw[:, s, :].bitcast(FP8X4),
+                rhs_scale=w2_sc_raw[:, s, :],
+                start=True,
+                stop=True,
+            )
         dc = []
         for d in range(PACK):
             dc_d = sb.tile([P, T], F32, name=f"dc{d}", align_bytes=64)

from contextlib import ExitStack

import concourse.mybir as mybir

K, T, E, C, H, N = 256, 1024, 8, 128, 512, 1024
FLOPS = 2 * N * H * T + 2 * H * K * E * C

F32 = mybir.dt.float32
BF16 = mybir.dt.bfloat16
I32 = mybir.dt.int32
U8 = mybir.dt.uint8
U16 = mybir.dt.uint16
FP8X4 = mybir.dt.float8_e4m3fn_x4
ALU = mybir.AluOpType
ACT = mybir.ActivationFunctionType

P = 128
PACK = 4
PASSES = N // (P * PACK)
BANK = 512
HALVES = T // BANK
CHUNK = 256
CHUNKS = E * C // CHUNK
EXPERTS_PER_CHUNK = CHUNK // C
K_BLOCKS = K // P
LIST_COLS = CHUNK // 16
GATHERS = ((0, CHUNK), (CHUNK, CHUNK), (2 * CHUNK, 2 * CHUNK))


def tile_moe_sdb_relu_kernel(
    tc, dy_words, dy_scales, w2t_words, w2t_scales, w1t_words, w1t_scales, a, gate, offs, out
):
    nc = tc.nc
    with ExitStack() as ctx:
        lists = ctx.enter_context(tc.tile_pool(name="lists", bufs=1))
        sb = ctx.enter_context(tc.tile_pool(name="sb", bufs=1))
        psum = ctx.enter_context(tc.psum_pool(name="psum", bufs=4))

        w2_sc_raw = sb.tile([P, PASSES, H], U8, name="w2_sc_raw", align_bytes=64)
        dy_sc = sb.tile([P, PASSES, T], U8, name="dy_sc", align_bytes=64)
        w1_sc = sb.tile([P, E, K], U8, name="w1_sc", align_bytes=64)
        nc.gpsimd.memset(w2_sc_raw[:].bitcast(I32), 0)
        nc.vector.memset(dy_sc[:].bitcast(I32), 0)
        nc.vector.memset(w1_sc[:].bitcast(I32), 0)

        w2_rows = w2t_scales.rearrange("s (q r) i -> r q s i", r=4)
        dy_rows = dy_scales.rearrange("s (q r) t -> r q s t", r=4)
        w1_rows = w1t_scales.rearrange("e o (q r) k -> r q (e o) k", r=4)

        def load_scale_rows(queue, plane, rows, r):
            queue.dma_start(plane[r:P:32, :, :].bitcast(I32), rows[r].bitcast(I32))

        def load_a(c):
            a_c = sb.tile([P, PACK, CHUNK], F32, name=f"a{c}", align_bytes=64)
            nc.sync.dma_start(a_c[:], a.rearrange("(p d) j -> p d j", d=PACK)[:, :, c * CHUNK : (c + 1) * CHUNK])
            return a_c

        def load_gate(n):
            first, width = GATHERS[n]
            gate_n = sb.tile([P, width], F32, name=f"gate{n}", align_bytes=64)
            nc.sync.dma_start(gate_n[:], gate[:, first : first + width])
            return gate_n

        def load_w1(g):
            w1_g = sb.tile([P, E // 2, K], I32, name=f"w1_{g}", align_bytes=64)
            words = w1t_words[g * (E // 2) : (g + 1) * (E // 2)]
            nc.sync.dma_start(w1_g[:], words.rearrange("e o p k d -> p (e o) (k d)").bitcast(I32))
            return w1_g

        offsets = lists.tile([P, E * C // 16], U16, name="offsets")
        nc.sync.dma_start(offsets[:], offs)
        w2_raw = sb.tile([P, PASSES, H], I32, name="w2_raw", align_bytes=64)
        nc.sync.dma_start(w2_raw[:], w2t_words.rearrange("s p i d -> p s (i d)").bitcast(I32))
        for r in range(4):
            load_scale_rows(nc.sync, w2_sc_raw, w2_rows, r)
        dy = sb.tile([P, PASSES, T], I32, name="dy", align_bytes=64)
        nc.sync.dma_start(dy[:], dy_words.rearrange("s p t d -> p s (t d)").bitcast(I32))
        for r in range(4):
            load_scale_rows(nc.sync, dy_sc, dy_rows, r)
        gates = [load_gate(0)]
        a_sb = [load_a(0)]
        gates.append(load_gate(1))
        a_sb.extend([load_a(1), load_a(2)])
        gates.append(load_gate(2))
        w1 = [load_w1(0)]
        for r in range(4):
            load_scale_rows(nc.sync, w1_sc, w1_rows, r)
        a_sb.append(load_a(3))
        w1.append(load_w1(1))

        w2 = []
        w2_sc = []
        for d in range(PACK):
            w2_d = sb.tile([P, PASSES, P], I32, name=f"w2_{d}", align_bytes=64)
            nc.vector.tensor_copy(w2_d[:], w2_raw[:].rearrange("p s (m d) -> p d s m", d=PACK)[:, d])
            w2.append(w2_d)
            w2_sc_d = sb.tile([P, PASSES, P], U8, name=f"w2_sc_{d}", align_bytes=64)
            nc.vector.tensor_copy(w2_sc_d[:], w2_sc_raw[:].rearrange("p s (m d) -> p d s m", d=PACK)[:, d])
            w2_sc.append(w2_sc_d)

        warm = psum.tile([P, BANK], F32, name="acc_dx")
        for s in range(PASSES):
            nc.tensor.matmul_mx(
                out=warm[:],
                lhsT=w2_raw[:, s, 0:P].bitcast(FP8X4),
                lhsT_scale=w2_sc_raw[:, s, 0:P],
                rhs=w2_raw[:, s, :].bitcast(FP8X4),
                rhs_scale=w2_sc_raw[:, s, :],
                start=True,
                stop=True,
            )
        dc = []
        for d in range(PACK):
            dc_d = sb.tile([P, T], F32, name=f"dc{d}", align_bytes=64)
            for h in range(HALVES):
                cols = slice(h * BANK, (h + 1) * BANK)
                acc = psum.tile([P, BANK], F32, name="acc")
                for s in range(PASSES):
                    nc.tensor.matmul_mx(
                        out=acc[:],
                        lhsT=w2[d][:, s, :].bitcast(FP8X4),
                        lhsT_scale=w2_sc[d][:, s, :],
                        rhs=dy[:, s, cols].bitcast(FP8X4),
                        rhs_scale=dy_sc[:, s, cols],
                        start=(s == 0),
                        stop=(s == PASSES - 1),
                    )
                nc.scalar.copy(dc_d[:, cols], acc[:])
            dc.append(dc_d)

        def woven(tile_ap):
            return tile_ap.rearrange("p (g i) d -> p g d i", i=4)

        def planes(tile_ap):
            return tile_ap.rearrange("p d (g i) -> p g d i", i=4)

        def make_sign(c):
            sgn = sb.tile([P, CHUNK, PACK], BF16, name=f"sgn{c}", align_bytes=64)
            nc.scalar.activation(woven(sgn[:]), planes(a_sb[c][:]), ACT.Sign)
            return sgn

        def make_mask(c, sgn):
            mask = sb.tile([P, CHUNK, PACK], BF16, name=f"mask{c}", align_bytes=64)
            nc.scalar.activation(mask[:], sgn[:], ACT.Relu)
            return mask

        gated = sb.tile([P, PACK, CHUNK], F32, name="gated", align_bytes=64)
        for d in range(PACK):
            nc.vector.scalar_tensor_tensor(gated[:, d, :], a_sb[0][:, d, :], 0.0, gates[0][:], ALU.is_gt, ALU.mult)
        gathered = []
        for n, (first, width) in enumerate(GATHERS):
            g_n = sb.tile([P, PACK, width], F32, name=f"gathered{n}", align_bytes=64)
            for d in range(PACK):
                nc.vector.tensor_tensor(
                    g_n[:, d, :],
                    dc[d][:].indirect(offsets[:, first // 16 : (first + width) // 16]),
                    gated[:, d, :] if n == 0 else gates[n][:],
                    ALU.mult,
                )
            gathered.extend(g_n[:, :, j : j + CHUNK] for j in range(0, width, CHUNK))

        out_sb = [sb.tile([P, T], F32, name=f"out_sb{kb}", align_bytes=64) for kb in range(K_BLOCKS)]

        def first_half(c, mask):
            rounded = sb.tile([P, CHUNK, PACK], BF16, name=f"rounded{c}", tag=f"rounded_then_dx{c}", align_bytes=64)
            nc.scalar.copy(woven(rounded[:]), planes(gathered[c]))
            da = rounded
            if mask is not None:
                da = sb.tile([P, CHUNK, PACK], BF16, name=f"da{c}", tag="da", align_bytes=64)
                engine = nc.vector if c == 1 else nc.gpsimd
                engine.tensor_tensor(da[:], rounded[:], mask[:], ALU.mult)
            codes = sb.tile([P, CHUNK], I32, name=f"codes{c}", align_bytes=64)
            scales = sb.tile([P, CHUNK], U8, name=f"scales{c}", align_bytes=64)
            nc.vector.quantize_mx(
                out=codes[:].bitcast(FP8X4), scales=scales[:], in_=da[:].rearrange("p j d -> p (j d)")
            )
            acc = psum.tile([P, K_BLOCKS, CHUNK], F32, name="acc_dx")
            for kb in range(K_BLOCKS):
                for u in range(EXPERTS_PER_CHUNK):
                    e = c * EXPERTS_PER_CHUNK + u
                    nc.tensor.matmul_mx(
                        out=acc[:, kb, u * C : (u + 1) * C],
                        lhsT=w1[e // (E // 2)][:, e % (E // 2), kb * P : (kb + 1) * P].bitcast(FP8X4),
                        lhsT_scale=w1_sc[:, e, kb * P : (kb + 1) * P],
                        rhs=codes[:, u * C : (u + 1) * C].bitcast(FP8X4),
                        rhs_scale=scales[:, u * C : (u + 1) * C],
                        start=True,
                        stop=True,
                    )
            return acc

        def second_half(c, acc):
            for kb in range(K_BLOCKS):
                tag = f"dx{c}" if kb == 0 else f"rounded_then_dx{(c + 1) % CHUNKS}"
                dx = sb.tile([P, CHUNK], F32, name=f"dx{c}_{kb}", tag=tag, align_bytes=64)
                nc.scalar.copy(dx[:], acc[:, kb, :])
                nc.vector.tensor_copy(out_sb[kb][:].indirect(offsets[:, c * LIST_COLS : (c + 1) * LIST_COLS]), dx[:])

        sgn1 = make_sign(1)
        sgn2 = make_sign(2)
        mask1 = make_mask(1, sgn1)
        accs = [first_half(0, None)]
        accs.append(first_half(1, mask1))
        accs.append(first_half(2, make_mask(2, sgn2)))
        second_half(0, accs[0])
        accs.append(first_half(3, make_mask(3, make_sign(3))))
        second_half(1, accs[1])
        second_half(2, accs[2])
        second_half(CHUNKS - 1, accs[CHUNKS - 1])
        for kb in range(K_BLOCKS):
            nc.sync.dma_start(out[kb * P : (kb + 1) * P, :], out_sb[kb][:])
